import numpy as np
import ml_dtypes


def mxq(x, axis, fmt="e4m3"):
    dtype, down = {"e4m3": (ml_dtypes.float8_e4m3fn, 7), "e5m2": (ml_dtypes.float8_e5m2, 14)}[fmt]
    v = np.moveaxis(np.asarray(x, np.float32).astype(ml_dtypes.bfloat16).astype(np.float64), axis, -1)
    blocks = v.reshape(v.shape[:-1] + (-1, 32))
    amax = np.abs(blocks).max(-1, keepdims=True)
    byte = np.maximum(np.where(amax > 0, np.frexp(amax)[1] - 1 + 127, 0) - down, 1)
    scale = np.exp2(byte - 127.0)
    codes = (blocks / scale).astype(np.float32).astype(dtype).astype(np.float64)
    return np.moveaxis((codes * scale).reshape(v.shape), -1, axis)


WIDE = False


def mx_kscale(k):
    if not WIDE:
        return np.ones(k)
    levels = np.array([10, -10, 5, -5, 0])
    if k % 512:
        return np.exp2(np.random.permutation(np.resize(levels, k // 32))).repeat(32)
    a = np.empty((k // 512, 16))
    for p in range(k // 512):
        a[p, :8] = np.random.permutation(np.resize(levels, 8))
        for g in range(8):
            far = levels[np.abs(levels - a[p, g]) >= 10]
            a[p, g + 8] = far[np.random.randint(len(far))]
    return np.exp2(a.ravel()).repeat(32)


def f64(x):
    return np.asarray(x).astype(np.float64)


def striped(idx):
    return np.tile(np.asarray(idx).reshape(-1, 16).T, (8, 1)).astype(np.uint16)


def unstriped(offs):
    return offs[:16].T.reshape(-1).astype(np.int64)


E2M1 = np.array([0.0, 0.5, 1.0, 1.5, 2.0, 3.0, 4.0, 6.0, -0.0, -0.5, -1.0, -1.5, -2.0, -3.0, -4.0, -6.0])


def pack_weight(w, fmt):
    k, n = w.shape
    w = f64(np.asarray(w, np.float32).astype(ml_dtypes.bfloat16)).reshape(k // 32, 32, n)
    amax = np.abs(w).max(1)
    if fmt == "e4m3":
        byte = np.frexp(amax)[1] - 1 + 127 - 7
    else:
        mant, ex = np.frexp(amax / 6.0)
        byte = np.where(mant > 0.5, ex, ex - 1) + 127
    byte = np.clip(np.where(amax > 0, byte, 1), 1, 254)
    scaled = (w * np.exp2(127.0 - byte)[:, None, :]).reshape(k, n).astype(np.float32)
    by_word = np.ascontiguousarray(scaled.reshape(k // 512, 128, 4, n).transpose(0, 1, 3, 2))
    if fmt == "e4m3":
        words = by_word.astype(ml_dtypes.float8_e4m3fn).view(np.uint8)
    else:
        c = by_word.astype(ml_dtypes.float4_e2m1fn).view(np.uint8) & 0xF
        words = (c[..., 0::2] | (c[..., 1::2] << 4)).reshape(k // 512, 128, 2 * n)
    return np.ascontiguousarray(words), np.ascontiguousarray(byte.astype(np.uint8).reshape(k // 512, 16, n))


def unpack_weight(words, scales, fmt):
    g, _, n = scales.shape
    words = np.ascontiguousarray(words).reshape(g, 128, n, -1)
    if fmt == "e4m3":
        vals = words.view(ml_dtypes.float8_e4m3fn).astype(np.float64)
    else:
        nib = np.empty((g, 128, n, 4), np.uint8)
        nib[..., 0::2] = words & 0xF
        nib[..., 1::2] = words >> 4
        vals = E2M1[nib]
    vals = vals * np.repeat(np.exp2(scales.astype(np.float64) - 127.0), 8, axis=1)[..., None]
    return vals.transpose(0, 1, 3, 2).reshape(g * 512, n)


D, T, I, Q, E, M = 512, 1024, 512, 512, 512, 1024


def setup_inputs():
    n = np.random.standard_normal
    idx = np.random.permutation(T)[:I]
    idx2 = np.random.permutation(T)[:I]
    idx3 = np.random.permutation(T)[:I]
    idx4 = np.random.permutation(M)[:I]
    fd = mx_kscale(D)
    fq = mx_kscale(Q)
    keysp = pack_weight(n((D, T)) / fd[:, None], "e4m3")
    return {
        "query": (n((D, Q)) * 1.2 / np.sqrt(D) * fd[:, None]).astype(np.float32),
        "keys_words": keysp[0],
        "keys_scales": keysp[1],
        "lam": (np.random.uniform(0.8, 1.8, (Q, 1))).astype(np.float32),
        "qs": (np.random.uniform(0.5, 2.0, (Q, 1)) * fq[:, None]).astype(np.float32),
        "msgs": (n((Q, E)) * 1 / np.sqrt(Q) / fq[:, None]).astype(np.float32),
        "old": (n((E, M)) * 1.0).astype(np.float32),
        "offs": striped(idx),
        "offs2": striped(idx2),
        "offs3": striped(idx3),
        "offs4": striped(idx4),
    }


def reference(query, keys_words, keys_scales, lam, qs, msgs, old, offs, offs2, offs3, offs4):
    idx = unstriped(offs)
    idx2 = unstriped(offs2)
    idx3 = unstriped(offs3)
    idx4 = unstriped(offs4)
    keysu = unpack_weight(keys_words, keys_scales, "e4m3")
    queryq = mxq(f64(query), 0, "e4m3")
    a = queryq.T @ keysu
    lo2 = np.minimum(a[:, idx], a[:, idx2])
    hi2 = np.maximum(a[:, idx], a[:, idx2])
    w = np.maximum(lo2, np.minimum(hi2, a[:, idx3])) * f64(lam)
    wq = w * f64(qs)
    msgsq = mxq(f64(msgs), 0, "e4m3")
    wqq = mxq(wq, 0, "e4m3")
    dl = msgsq.T @ wqq
    df = np.zeros((E, M))
    df[:, idx4] = dl
    y = f64(old) + df
    return y

@@ -1,0 +1,187 @@
+from contextlib import ExitStack
+
+import concourse.mybir as mybir
+
+D, T, I, Q, E, M = 512, 1024, 512, 512, 512, 1024
+FLOPS = 2 * D * Q * T + 2 * Q * E * I
+
+F32 = mybir.dt.float32
+BF16 = mybir.dt.bfloat16
+U32 = mybir.dt.uint32
+I32 = mybir.dt.int32
+U16 = mybir.dt.uint16
+U8 = mybir.dt.uint8
+FP8X4 = mybir.dt.float8_e4m3fn_x4
+ALU = mybir.AluOpType
+COPY = mybir.ActivationFunctionType.Copy
+P = 128
+H = 256
+PLAN = "P:mm0 P:mm1 S:ev00 V:ev01 S:ev10 S:ev11 P:mm2 P:mm3 V:gx00 V:gy00 V:gz00 S:gx10 S:gy10 S:gz10 V:ev20 V:ev21 V:hi00 V:lo00 V:mi00 S:gx20 S:gy20 S:gz20 S:ev30 S:ev31 V:ci V:ww00 S:gx30 S:gy30 S:gz30 V:qm V:hi10 V:lo10 V:mi10 S:gx01 S:gy01 S:gx11 S:gy11 S:gz01 S:gz11 V:hi01 V:ww10 V:lo01 V:sc0 V:mi01 V:qw0 P:m20 V:ww01 S:gx21 S:gy21 S:gx31 S:gy31 S:gz21 S:gz31 V:hi11a V:hi11b V:lo11a V:mi11a V:lo11b V:mi11b V:ww11a V:ww11b V:sc1a V:sc1b V:qw1a V:qw1b P:m21 S:dl00 S:st00 S:st10 S:dl10 V:st20 S:dl01 S:st01 S:dl11 S:st11 V:st30 G:ad0a V:st21 S:st31 V:ad2 V:ad0b V:ad1 V:ad3a V:ad3b"
+
+
+def tile_attend_middle_deliveredplanes_lean_kernel(tc, query, keys_words, keys_scales, lam, qs, msgs, old, offs, offs2, offs3, offs4, out):
+    nc = tc.nc
+    with ExitStack() as ctx:
+        keep = ctx.enter_context(tc.tile_pool(name="keep", bufs=1))
+        psa = ctx.enter_context(tc.psum_pool(name="psa", bufs=4))
+        psd = ctx.enter_context(tc.psum_pool(name="psd", bufs=4))
+
+        lists = [keep.tile([P, I // 16], U16, name="list%d" % n) for n in range(4)]
+        k_words = keep.tile([P, T], U32, align_bytes=64)
+        k_scales = keep.tile([P, T], U8, align_bytes=64)
+        lam_sb = keep.tile([P, 4], F32)
+        qs_sb = keep.tile([P, 4], F32)
+        c_sb = keep.tile([P, 4], F32)
+        q_raw = [keep.tile([P, 4, 256], F32, name="q_raw%d" % n) for n in range(2)]
+        q_il = keep.tile([P, 4, 128, 4], BF16, align_bytes=64)
+        q_words = keep.tile([P, Q], U32, align_bytes=64)
+        q_scales = keep.tile([P, Q], U8, align_bytes=64)
+        m_raw = keep.tile([P, 4, E], F32)
+        m_il = keep.tile([P, E, 4], BF16, align_bytes=64)
+        m_words = keep.tile([P, E], U32, align_bytes=64)
+        m_scales = keep.tile([P, E], U8, align_bytes=64)
+        olds = [keep.tile([P, M], F32, name="old%d" % n) for n in range(4)]
+        wins = [keep.tile([P, M], F32, name="win%d" % n) for n in range(4)]
+        a_sb = [keep.tile([P, T], F32, name="a%d" % n) for n in range(4)]
+        g = {(c, k, h): keep.tile([P, 2, H], F32, name="g%s%d%d" % (c, k, h)) for c in "xyz" for k in range(2) for h in range(2)}
+        lo = {(k, h): keep.tile([P, 2, H], F32, name="lo%d%d" % (k, h)) for k in range(2) for h in range(2)}
+        hi = {(k, h): keep.tile([P, 2, H], F32, name="hi%d%d" % (k, h)) for k in range(2) for h in range(2)}
+        w = [keep.tile([P, 4, H], F32, name="w%d" % h) for h in range(2)]
+        w_il = [keep.tile([P, H, 4], BF16, name="w_il%d" % h, align_bytes=64) for h in range(2)]
+        w_words = [keep.tile([P, H], U32, name="w_words%d" % h, align_bytes=64) for h in range(2)]
+        w_scales = [keep.tile([P, H], U8, name="w_scales%d" % h, align_bytes=64) for h in range(2)]
+        dl = {(k, h): keep.tile([P, 2, H], F32, name="dl%d%d" % (k, h)) for k in range(2) for h in range(2)}
+
+        nc.vector.memset(k_scales[:].bitcast(I32), 0)
+        nc.scalar.dma_start(out=lam_sb[:], in_=lam.rearrange("(p j) o -> p (j o)", j=4))
+        nc.scalar.dma_start(out=qs_sb[:], in_=qs.rearrange("(p j) o -> p (j o)", j=4))
+        qv = query.rearrange("(p j) q -> p j q", j=4)
+        for n in range(2):
+            nc.sync.dma_start(out=q_raw[n][:], in_=qv[:, :, 256 * n : 256 * (n + 1)])
+        nc.sync.dma_start(out=k_words[:].bitcast(I32), in_=keys_words[0].rearrange("p n t -> p (n t)").bitcast(I32))
+        for quad in range(4):
+            nc.scalar.dma_start(out=k_scales[32 * quad : 32 * quad + 4, :].bitcast(I32), in_=keys_scales[0, 4 * quad : 4 * quad + 4, :].bitcast(I32))
+        for n, src in enumerate((offs, offs2, offs3)):
+            nc.sync.dma_start(lists[n][:], src)
+        nc.sync.dma_start(out=m_raw[:], in_=msgs.rearrange("(p j) e -> p j e", j=4))
+        nc.sync.dma_start(lists[3][:], offs4)
+        for e in range(4):
+            nc.sync.dma_start(out=olds[e][:], in_=old[P * e : P * (e + 1), :])
+        for e in range(4):
+            nc.vector.memset(wins[e][:], 0.0)
+        for r in range(4):
+            nc.scalar.activation(out=c_sb[:, r : r + 1], in_=lam_sb[:, r : r + 1], func=COPY, scale=qs_sb[:, r : r + 1])
+
+        for n in range(2):
+            nc.vector.tensor_copy(
+                out=q_il[:, :, 64 * n : 64 * (n + 1), :].rearrange("p t m j -> p m j t"),
+                in_=q_raw[n][:].rearrange("p j (m t) -> p m j t", t=4),
+            )
+        for t in range(4):
+            nc.vector.quantize_mx(
+                out=q_words[:, P * t : P * (t + 1)].bitcast(FP8X4),
+                scales=q_scales[:, P * t : P * (t + 1)],
+                in_=q_il[:, t, :, :].rearrange("p m j -> p (m j)"),
+            )
+
+        banks = {}
+        dbanks = {}
+        eng = {"V": nc.vector, "S": nc.scalar, "G": nc.gpsimd}
+
+        def copy(who, dst, src):
+            if who == "S":
+                nc.scalar.copy(out=dst, in_=src)
+            else:
+                eng[who].tensor_copy(out=dst, in_=src)
+
+        def icopy(who, dst, src):
+            if who == "S":
+                nc.scalar.activation(out=dst, in_=src, func=COPY)
+            else:
+                nc.vector.tensor_copy(out=dst, in_=src)
+
+        for tok in PLAN.split():
+            who, name = tok.split(":")
+            kind = name[:2]
+            part = {"a": (0, 1), "b": (1, 2)}.get(name[-1], (0, 2))
+            sl = slice(part[0] * H // 2, part[1] * H // 2)
+            ns = sl.stop - sl.start
+            if kind == "mm":
+                r = int(name[2])
+                for b in range(2):
+                    bank = psa.tile([P, 512], F32, name="abank")
+                    banks[r, b] = bank
+                    nc.tensor.matmul_mx(
+                        out=bank[:],
+                        lhsT=q_words[:, P * r : P * (r + 1)].bitcast(FP8X4),
+                        lhsT_scale=q_scales[:, P * r : P * (r + 1)],
+                        rhs=k_words[:, 512 * b : 512 * (b + 1)].bitcast(FP8X4),
+                        rhs_scale=k_scales[:, 512 * b : 512 * (b + 1)],
+                        start=True,
+                        stop=True,
+                    )
+            elif kind == "ev":
+                r, b = int(name[2]), int(name[3])
+                copy(who, a_sb[r][:, 512 * b : 512 * (b + 1)], banks[r, b][:])
+            elif kind in ("gx", "gy", "gz"):
+                r, h = int(name[2]), int(name[3])
+                n = "xyz".index(kind[1])
+                icopy(who, g[kind[1], r // 2, h][:, r % 2, :], a_sb[r][:].indirect(lists[n][:, 16 * h : 16 * (h + 1)]))
+            elif kind in ("hi", "lo"):
+                k, h = int(name[2]), int(name[3])
+                nc.vector.tensor_tensor(
+                    out=(hi if kind == "hi" else lo)[k, h][:, :, sl],
+                    in0=g["x", k, h][:, :, sl],
+                    in1=g["y", k, h][:, :, sl],
+                    op=ALU.max if kind == "hi" else ALU.min,
+                )
+            elif kind == "mi":
+                k, h = int(name[2]), int(name[3])
+                nc.vector.tensor_tensor(out=hi[k, h][:, :, sl], in0=hi[k, h][:, :, sl], in1=g["z", k, h][:, :, sl], op=ALU.min)
+            elif kind == "ww":
+                k, h = int(name[2]), int(name[3])
+                nc.vector.tensor_tensor(out=w[h][:, 2 * k : 2 * k + 2, sl], in0=lo[k, h][:, :, sl], in1=hi[k, h][:, :, sl], op=ALU.max)
+            elif kind == "sc":
+                h = int(name[2])
+                nc.vector.tensor_tensor(
+                    out=w_il[h][:, sl, :].rearrange("p (c i) t -> p c t i", i=4),
+                    in0=w[h][:, :, sl].rearrange("p t (c i) -> p c t i", i=4),
+                    in1=c_sb[:].unsqueeze(1).unsqueeze(3).to_broadcast([P, ns // 4, 4, 4]),
+                    op=ALU.mult,
+                )
+            elif kind == "qw":
+                h = int(name[2])
+                nc.vector.quantize_mx(out=w_words[h][:, sl].bitcast(FP8X4), scales=w_scales[h][:, sl], in_=w_il[h][:, sl, :].rearrange("p i t -> p (i t)"))
+            elif kind == "ci":
+                es = slice(2 * sl.start, 2 * sl.stop)
+                copy(who, m_il[:, es, :].rearrange("p (c i) j -> p c j i", i=4), m_raw[:, :, es].rearrange("p j (c i) -> p c j i", i=4))
+            elif kind == "qm":
+                nc.vector.quantize_mx(out=m_words[:].bitcast(FP8X4), scales=m_scales[:], in_=m_il[:].rearrange("p e j -> p (e j)"))
+            elif kind == "m2":
+                h = int(name[2])
+                for k in range(2):
+                    bank = psd.tile([P, 2, H], F32, name="dbank")
+                    dbanks[k, h] = bank
+                    for u in range(2):
+                        e = 2 * k + u
+                        nc.tensor.matmul_mx(
+                            out=bank[:, u, :],
+                            lhsT=m_words[:, P * e : P * (e + 1)].bitcast(FP8X4),
+                            lhsT_scale=m_scales[:, P * e : P * (e + 1)],
+                            rhs=w_words[h][:].bitcast(FP8X4),
+                            rhs_scale=w_scales[h][:],
+                            start=True,
+                            stop=True,
+                        )
+            elif kind == "dl":
+                k, h = int(name[2]), int(name[3])
+                copy(who, dl[k, h][:], dbanks[k, h][:])
+            elif kind == "st":
+                e, h = int(name[2]), int(name[3])
+                a, b = (0, 16) if len(name) == 4 else ((0, 8) if name[4] == "a" else (8, 16))
+                icopy(who, wins[e][:].indirect(lists[3][:, 16 * h + a : 16 * h + b]), dl[e // 2, h][:, e % 2, 16 * a : 16 * b])
+            elif kind == "ad":
+                e = int(name[2])
+                a, b = (0, M) if len(name) == 3 else ((0, M // 2) if name[3] == "a" else (M // 2, M))
+                eng[who].tensor_tensor(out=olds[e][:, a:b], in0=olds[e][:, a:b], in1=wins[e][:, a:b], op=ALU.add)
+                nc.sync.dma_start(out=out[P * e : P * (e + 1), a:b], in_=olds[e][:, a:b])

@@ -16,7 +16,7 @@ ALU = mybir.AluOpType
 COPY = mybir.ActivationFunctionType.Copy
 P = 128
 H = 256
-PLAN = "P:mm0 P:mm1 S:ev00 V:ev01 S:ev10 S:ev11 P:mm2 P:mm3 V:gx00 V:gy00 V:gz00 S:gx10 S:gy10 S:gz10 V:ev20 V:ev21 V:hi00 V:lo00 V:mi00 S:gx20 S:gy20 S:gz20 S:ev30 S:ev31 V:ci V:ww00 S:gx30 S:gy30 S:gz30 V:qm V:hi10 V:lo10 V:mi10 S:gx01 S:gy01 S:gx11 S:gy11 S:gz01 S:gz11 V:hi01 V:ww10 V:lo01 V:sc0 V:mi01 V:qw0 P:m20 V:ww01 S:gx21 S:gy21 S:gx31 S:gy31 S:gz21 S:gz31 V:hi11a V:hi11b V:lo11a V:mi11a V:lo11b V:mi11b V:ww11a V:ww11b V:sc1a V:sc1b V:qw1a V:qw1b P:m21 S:dl00 S:st00 S:st10 S:dl10 V:st20 S:dl01 S:st01 S:dl11 S:st11 V:st30 G:ad0a V:st21 S:st31 V:ad2 V:ad0b V:ad1 V:ad3a V:ad3b"
+PLAN = "P:mm0 P:mm1 S:ev00 V:ev01 S:ev10 S:ev11 P:mm2 P:mm3 V:gx00 V:gy00 V:gz00 S:gx10 S:gy10 S:gz10 V:ev20 V:ev21 V:hi00 V:lo00 V:mi00 S:gx20 S:gy20 S:ev30 S:ev31 V:gz20 V:ww00 V:ci V:qm S:gx30 S:gy30 S:gz30 V:ts00 V:ts10 V:hi10 V:lo10 V:mi10a V:mi10b V:ww10a V:ww10b V:ts20a V:ts30a V:ts20b V:ts30b V:il0a V:il0b V:qw0a V:qw0b P:m20 S:gx01 S:gy01 S:gx11 S:gy11 S:gz01 S:gz11 V:hi01 V:lo01 V:mi01 S:gx21 S:gy21 S:gx31 S:gy31 S:gz21 S:gz31 V:ww01 V:ts01 V:ts11 V:hi11 V:lo11 V:mi11a V:mi11b V:ww11a V:ww11b V:ts21a V:ts31a V:ts21b V:ts31b V:il1a V:il1b V:qw1a V:qw1b P:m21 S:dl00 S:st00 S:st10 S:dl10 S:st20 V:st30 S:dl01 S:dl11 S:st01 V:st21 S:st11 V:ad2 S:st31 V:ad0 V:ad1 V:ad3a V:ad3b"
 
 
 def tile_attend_middle_deliveredplanes_lean_kernel(tc, query, keys_words, keys_scales, lam, qs, msgs, old, offs, offs2, offs3, offs4, out):
@@ -32,7 +32,7 @@ def tile_attend_middle_deliveredplanes_lean_kernel(tc, query, keys_words, keys_s
         lam_sb = keep.tile([P, 4], F32)
         qs_sb = keep.tile([P, 4], F32)
         c_sb = keep.tile([P, 4], F32)
-        q_raw = [keep.tile([P, 4, 256], F32, name="q_raw%d" % n) for n in range(2)]
+        q_raw = keep.tile([P, 4, Q], F32)
         q_il = keep.tile([P, 4, 128, 4], BF16, align_bytes=64)
         q_words = keep.tile([P, Q], U32, align_bytes=64)
         q_scales = keep.tile([P, Q], U8, align_bytes=64)
@@ -47,20 +47,19 @@ def tile_attend_middle_deliveredplanes_lean_kernel(tc, query, keys_words, keys_s
         lo = {(k, h): keep.tile([P, 2, H], F32, name="lo%d%d" % (k, h)) for k in range(2) for h in range(2)}
         hi = {(k, h): keep.tile([P, 2, H], F32, name="hi%d%d" % (k, h)) for k in range(2) for h in range(2)}
         w = [keep.tile([P, 4, H], F32, name="w%d" % h) for h in range(2)]
+        w_bf = [keep.tile([P, 4, H], BF16, name="w_bf%d" % h) for h in range(2)]
         w_il = [keep.tile([P, H, 4], BF16, name="w_il%d" % h, align_bytes=64) for h in range(2)]
         w_words = [keep.tile([P, H], U32, name="w_words%d" % h, align_bytes=64) for h in range(2)]
         w_scales = [keep.tile([P, H], U8, name="w_scales%d" % h, align_bytes=64) for h in range(2)]
         dl = {(k, h): keep.tile([P, 2, H], F32, name="dl%d%d" % (k, h)) for k in range(2) for h in range(2)}
 
-        nc.vector.memset(k_scales[:].bitcast(I32), 0)
-        nc.scalar.dma_start(out=lam_sb[:], in_=lam.rearrange("(p j) o -> p (j o)", j=4))
-        nc.scalar.dma_start(out=qs_sb[:], in_=qs.rearrange("(p j) o -> p (j o)", j=4))
-        qv = query.rearrange("(p j) q -> p j q", j=4)
-        for n in range(2):
-            nc.sync.dma_start(out=q_raw[n][:], in_=qv[:, :, 256 * n : 256 * (n + 1)])
-        nc.sync.dma_start(out=k_words[:].bitcast(I32), in_=keys_words[0].rearrange("p n t -> p (n t)").bitcast(I32))
+        nc.gpsimd.memset(k_scales[:].bitcast(I32), 0)
+        nc.sync.dma_start(out=q_raw[:], in_=query.rearrange("(p j) q -> p j q", j=4))
         for quad in range(4):
-            nc.scalar.dma_start(out=k_scales[32 * quad : 32 * quad + 4, :].bitcast(I32), in_=keys_scales[0, 4 * quad : 4 * quad + 4, :].bitcast(I32))
+            nc.sync.dma_start(out=k_scales[32 * quad : 32 * quad + 4, :].bitcast(I32), in_=keys_scales[0, 4 * quad : 4 * quad + 4, :].bitcast(I32))
+        nc.sync.dma_start(out=k_words[:].bitcast(I32), in_=keys_words[0].rearrange("p n t -> p (n t)").bitcast(I32))
+        nc.sync.dma_start(out=lam_sb[:], in_=lam.rearrange("(p j) o -> p (j o)", j=4))
+        nc.sync.dma_start(out=qs_sb[:], in_=qs.rearrange("(p j) o -> p (j o)", j=4))
         for n, src in enumerate((offs, offs2, offs3)):
             nc.sync.dma_start(lists[n][:], src)
         nc.sync.dma_start(out=m_raw[:], in_=msgs.rearrange("(p j) e -> p j e", j=4))
@@ -69,14 +68,10 @@ def tile_attend_middle_deliveredplanes_lean_kernel(tc, query, keys_words, keys_s
             nc.sync.dma_start(out=olds[e][:], in_=old[P * e : P * (e + 1), :])
         for e in range(4):
             nc.vector.memset(wins[e][:], 0.0)
-        for r in range(4):
-            nc.scalar.activation(out=c_sb[:, r : r + 1], in_=lam_sb[:, r : r + 1], func=COPY, scale=qs_sb[:, r : r + 1])
-
-        for n in range(2):
-            nc.vector.tensor_copy(
-                out=q_il[:, :, 64 * n : 64 * (n + 1), :].rearrange("p t m j -> p m j t"),
-                in_=q_raw[n][:].rearrange("p j (m t) -> p m j t", t=4),
-            )
+        q_dst = q_il[:].rearrange("p t m j -> p m t j")
+        q_src = q_raw[:].rearrange("p j (m t) -> p m t j", t=4)
+        nc.vector.tensor_copy(out=q_dst[:, :84], in_=q_src[:, :84])
+        nc.scalar.activation(out=q_dst[:, 84:], in_=q_src[:, 84:], func=COPY)
         for t in range(4):
             nc.vector.quantize_mx(
                 out=q_words[:, P * t : P * (t + 1)].bitcast(FP8X4),
@@ -149,6 +144,12 @@ def tile_attend_middle_deliveredplanes_lean_kernel(tc, query, keys_words, keys_s
                     in1=c_sb[:].unsqueeze(1).unsqueeze(3).to_broadcast([P, ns // 4, 4, 4]),
                     op=ALU.mult,
                 )
+            elif kind == "ts":
+                r, h = int(name[2]), int(name[3])
+                nc.vector.tensor_scalar(out=w_bf[h][:, r, sl], in0=w[h][:, r, sl], scalar1=lam_sb[:, r : r + 1], scalar2=qs_sb[:, r : r + 1], op0=ALU.mult, op1=ALU.mult)
+            elif kind == "il":
+                h = int(name[2])
+                nc.vector.tensor_copy(out=w_il[h][:, sl, :].rearrange("p (c i) t -> p c t i", i=4), in_=w_bf[h][:, :, sl].rearrange("p t (c i) -> p c t i", i=4))
             elif kind == "qw":
                 h = int(name[2])
                 nc.vector.quantize_mx(out=w_words[h][:, sl].bitcast(FP8X4), scales=w_scales[h][:, sl], in_=w_il[h][:, sl, :].rearrange("p i t -> p (i t)"))

@@ -14,175 +14,223 @@ U8 = mybir.dt.uint8
 FP8X4 = mybir.dt.float8_e4m3fn_x4
 ALU = mybir.AluOpType
 COPY = mybir.ActivationFunctionType.Copy
+
 P = 128
-H = 256
-PLAN = "P:mm0 P:mm1 S:ev00 V:ev01 S:ev10 S:ev11 P:mm2 P:mm3 V:gx00 V:gy00 V:gz00 S:gx10 S:gy10 S:gz10 V:ev20 V:ev21 V:hi00 V:lo00 V:mi00 S:gx20 S:gy20 S:ev30 S:ev31 V:gz20 V:ww00 V:ci V:qm S:gx30 S:gy30 S:gz30 V:ts00 V:ts10 V:hi10 V:lo10 V:mi10a V:mi10b V:ww10a V:ww10b V:ts20a V:ts30a V:ts20b V:ts30b V:il0a V:il0b V:qw0a V:qw0b P:m20 S:gx01 S:gy01 S:gx11 S:gy11 S:gz01 S:gz11 V:hi01 V:lo01 V:mi01 S:gx21 S:gy21 S:gx31 S:gy31 S:gz21 S:gz31 V:ww01 V:ts01 V:ts11 V:hi11 V:lo11 V:mi11a V:mi11b V:ww11a V:ww11b V:ts21a V:ts31a V:ts21b V:ts31b V:il1a V:il1b V:qw1a V:qw1b P:m21 S:dl00 S:st00 S:st10 S:dl10 S:st20 V:st30 S:dl01 S:dl11 S:st01 V:st21 S:st11 V:ad2 S:st31 V:ad0 V:ad1 V:ad3a V:ad3b"
+PACK = 4
+BANK = 512
+BANKS = 8
+E_TILES = E // P
+HALF = I // 2
+LIST_COLS = HALF // 16
+Q_GROUPS_VECTOR = 84
 
 
 def tile_attend_middle_deliveredplanes_lean_kernel(tc, query, keys_words, keys_scales, lam, qs, msgs, old, offs, offs2, offs3, offs4, out):
     nc = tc.nc
+    halves = range(2)
+    pairs = range(2)
+    whole = slice(0, HALF)
+    quarters = (slice(0, HALF // 2), slice(HALF // 2, HALF))
+
     with ExitStack() as ctx:
         keep = ctx.enter_context(tc.tile_pool(name="keep", bufs=1))
-        psa = ctx.enter_context(tc.psum_pool(name="psa", bufs=4))
-        psd = ctx.enter_context(tc.psum_pool(name="psd", bufs=4))
+        psum = ctx.enter_context(tc.psum_pool(name="psum", bufs=BANKS))
 
-        lists = [keep.tile([P, I // 16], U16, name="list%d" % n) for n in range(4)]
+        pick = [keep.tile([P, I // 16], U16, name="pick%d" % n) for n in range(3)]
+        place = keep.tile([P, I // 16], U16)
         k_words = keep.tile([P, T], U32, align_bytes=64)
         k_scales = keep.tile([P, T], U8, align_bytes=64)
-        lam_sb = keep.tile([P, 4], F32)
-        qs_sb = keep.tile([P, 4], F32)
-        c_sb = keep.tile([P, 4], F32)
-        q_raw = keep.tile([P, 4, Q], F32)
-        q_il = keep.tile([P, 4, 128, 4], BF16, align_bytes=64)
+        lam_sb = keep.tile([P, PACK], F32)
+        qs_sb = keep.tile([P, PACK], F32)
+        q_raw = keep.tile([P, PACK, Q], F32)
+        q_packed = keep.tile([P, PACK, P, PACK], BF16, align_bytes=64)
         q_words = keep.tile([P, Q], U32, align_bytes=64)
         q_scales = keep.tile([P, Q], U8, align_bytes=64)
-        m_raw = keep.tile([P, 4, E], F32)
-        m_il = keep.tile([P, E, 4], BF16, align_bytes=64)
+        m_raw = [keep.tile([P, PACK, E // 2], F32, name="m_raw%d" % n) for n in range(2)]
+        m_packed = keep.tile([P, E, PACK], BF16, align_bytes=64)
         m_words = keep.tile([P, E], U32, align_bytes=64)
         m_scales = keep.tile([P, E], U8, align_bytes=64)
-        olds = [keep.tile([P, M], F32, name="old%d" % n) for n in range(4)]
-        wins = [keep.tile([P, M], F32, name="win%d" % n) for n in range(4)]
-        a_sb = [keep.tile([P, T], F32, name="a%d" % n) for n in range(4)]
-        g = {(c, k, h): keep.tile([P, 2, H], F32, name="g%s%d%d" % (c, k, h)) for c in "xyz" for k in range(2) for h in range(2)}
-        lo = {(k, h): keep.tile([P, 2, H], F32, name="lo%d%d" % (k, h)) for k in range(2) for h in range(2)}
-        hi = {(k, h): keep.tile([P, 2, H], F32, name="hi%d%d" % (k, h)) for k in range(2) for h in range(2)}
-        w = [keep.tile([P, 4, H], F32, name="w%d" % h) for h in range(2)]
-        w_bf = [keep.tile([P, 4, H], BF16, name="w_bf%d" % h) for h in range(2)]
-        w_il = [keep.tile([P, H, 4], BF16, name="w_il%d" % h, align_bytes=64) for h in range(2)]
-        w_words = [keep.tile([P, H], U32, name="w_words%d" % h, align_bytes=64) for h in range(2)]
-        w_scales = [keep.tile([P, H], U8, name="w_scales%d" % h, align_bytes=64) for h in range(2)]
-        dl = {(k, h): keep.tile([P, 2, H], F32, name="dl%d%d" % (k, h)) for k in range(2) for h in range(2)}
+        result = [keep.tile([P, M], F32, name="result%d" % e) for e in range(E_TILES)]
+        window = [keep.tile([P, M], F32, name="window%d" % e) for e in range(E_TILES)]
+        a_sb = [keep.tile([P, T], F32, name="a%d" % r) for r in range(PACK)]
+        picked = {(n, k, h): keep.tile([P, 2, HALF], F32, name="picked%d%d%d" % (n, k, h)) for n in range(3) for k in pairs for h in halves}
+        lo = {(k, h): keep.tile([P, 2, HALF], F32, name="lo%d%d" % (k, h)) for k in pairs for h in halves}
+        hi = {(k, h): keep.tile([P, 2, HALF], F32, name="hi%d%d" % (k, h)) for k in pairs for h in halves}
+        median = [keep.tile([P, PACK, HALF], F32, name="median%d" % h) for h in halves]
+        wq = [keep.tile([P, PACK, HALF], BF16, name="wq%d" % h) for h in halves]
+        w_packed = [keep.tile([P, HALF, PACK], BF16, name="w_packed%d" % h, align_bytes=64) for h in halves]
+        w_words = [keep.tile([P, HALF], U32, name="w_words%d" % h, align_bytes=64) for h in halves]
+        w_scales = [keep.tile([P, HALF], U8, name="w_scales%d" % h, align_bytes=64) for h in halves]
+        dl = {(k, h): keep.tile([P, 2, HALF], F32, name="dl%d%d" % (k, h)) for k in pairs for h in halves}
+        dl_bank = {}
 
         nc.gpsimd.memset(k_scales[:].bitcast(I32), 0)
-        nc.sync.dma_start(out=q_raw[:], in_=query.rearrange("(p j) q -> p j q", j=4))
+        nc.sync.dma_start(out=q_raw[:], in_=query.rearrange("(p j) q -> p j q", j=PACK))
         for quad in range(4):
-            nc.sync.dma_start(out=k_scales[32 * quad : 32 * quad + 4, :].bitcast(I32), in_=keys_scales[0, 4 * quad : 4 * quad + 4, :].bitcast(I32))
+            nc.sync.dma_start(
+                out=k_scales[32 * quad : 32 * quad + 4, :].bitcast(I32),
+                in_=keys_scales[0, 4 * quad : 4 * quad + 4, :].bitcast(I32),
+            )
         nc.sync.dma_start(out=k_words[:].bitcast(I32), in_=keys_words[0].rearrange("p n t -> p (n t)").bitcast(I32))
-        nc.sync.dma_start(out=lam_sb[:], in_=lam.rearrange("(p j) o -> p (j o)", j=4))
-        nc.sync.dma_start(out=qs_sb[:], in_=qs.rearrange("(p j) o -> p (j o)", j=4))
-        for n, src in enumerate((offs, offs2, offs3)):
-            nc.sync.dma_start(lists[n][:], src)
-        nc.sync.dma_start(out=m_raw[:], in_=msgs.rearrange("(p j) e -> p j e", j=4))
-        nc.sync.dma_start(lists[3][:], offs4)
-        for e in range(4):
-            nc.sync.dma_start(out=olds[e][:], in_=old[P * e : P * (e + 1), :])
-        for e in range(4):
-            nc.vector.memset(wins[e][:], 0.0)
-        q_dst = q_il[:].rearrange("p t m j -> p m t j")
-        q_src = q_raw[:].rearrange("p j (m t) -> p m t j", t=4)
-        nc.vector.tensor_copy(out=q_dst[:, :84], in_=q_src[:, :84])
-        nc.scalar.activation(out=q_dst[:, 84:], in_=q_src[:, 84:], func=COPY)
-        for t in range(4):
+        for tile, offsets in zip(pick, (offs, offs2, offs3)):
+            nc.sync.dma_start(tile[:], offsets)
+        m_rows = msgs.rearrange("(p j) e -> p j e", j=PACK)
+        for n in range(2):
+            nc.sync.dma_start(out=m_raw[n][:], in_=m_rows[:, :, n * E // 2 : (n + 1) * E // 2])
+        nc.sync.dma_start(out=lam_sb[:], in_=lam.rearrange("(p r) o -> p (r o)", r=PACK))
+        nc.sync.dma_start(out=qs_sb[:], in_=qs.rearrange("(p r) o -> p (r o)", r=PACK))
+        nc.sync.dma_start(place[:], offs4)
+        for e in range(E_TILES):
+            nc.sync.dma_start(out=result[e][:], in_=old[P * e : P * (e + 1), :])
+        for e in range(E_TILES):
+            nc.vector.memset(window[e][:], 0.0)
+
+        q_to = q_packed[:].rearrange("p r s j -> p s r j")
+        q_from = q_raw[:].rearrange("p j (s r) -> p s r j", r=PACK)
+        nc.vector.tensor_copy(out=q_to[:, :Q_GROUPS_VECTOR], in_=q_from[:, :Q_GROUPS_VECTOR])
+        nc.scalar.activation(out=q_to[:, Q_GROUPS_VECTOR:], in_=q_from[:, Q_GROUPS_VECTOR:], func=COPY)
+        for r in range(PACK):
             nc.vector.quantize_mx(
-                out=q_words[:, P * t : P * (t + 1)].bitcast(FP8X4),
-                scales=q_scales[:, P * t : P * (t + 1)],
-                in_=q_il[:, t, :, :].rearrange("p m j -> p (m j)"),
+                out=q_words[:, P * r : P * (r + 1)].bitcast(FP8X4),
+                scales=q_scales[:, P * r : P * (r + 1)],
+                in_=q_packed[:, r, :, :].rearrange("p s j -> p (s j)"),
             )
 
-        banks = {}
-        dbanks = {}
-        eng = {"V": nc.vector, "S": nc.scalar, "G": nc.gpsimd}
+        def product(bank, lhs_words, lhs_scales, rhs_words, rhs_scales):
+            nc.tensor.matmul_mx(
+                out=bank,
+                lhsT=lhs_words.bitcast(FP8X4),
+                lhsT_scale=lhs_scales,
+                rhs=rhs_words.bitcast(FP8X4),
+                rhs_scale=rhs_scales,
+                start=True,
+                stop=True,
+            )
 
-        def copy(who, dst, src):
-            if who == "S":
-                nc.scalar.copy(out=dst, in_=src)
+        def move(engine, to, source):
+            if engine is nc.scalar:
+                nc.scalar.activation(out=to, in_=source, func=COPY)
             else:
-                eng[who].tensor_copy(out=dst, in_=src)
+                nc.vector.tensor_copy(out=to, in_=source)
 
-        def icopy(who, dst, src):
-            if who == "S":
-                nc.scalar.activation(out=dst, in_=src, func=COPY)
-            else:
-                nc.vector.tensor_copy(out=dst, in_=src)
+        def scores(r):
+            rows = slice(P * r, P * (r + 1))
+            banks = []
+            for b in range(T // BANK):
+                tokens = slice(BANK * b, BANK * (b + 1))
+                bank = psum.tile([P, BANK], F32, name="bank")
+                product(bank[:], q_words[:, rows], q_scales[:, rows], k_words[:, tokens], k_scales[:, tokens])
+                banks.append(bank)
+            nc.scalar.copy(out=a_sb[r][:, :BANK], in_=banks[0][:])
+            nc.vector.tensor_copy(out=a_sb[r][:, BANK:], in_=banks[1][:])
 
-        for tok in PLAN.split():
-            who, name = tok.split(":")
-            kind = name[:2]
-            part = {"a": (0, 1), "b": (1, 2)}.get(name[-1], (0, 2))
-            sl = slice(part[0] * H // 2, part[1] * H // 2)
-            ns = sl.stop - sl.start
-            if kind == "mm":
-                r = int(name[2])
-                for b in range(2):
-                    bank = psa.tile([P, 512], F32, name="abank")
-                    banks[r, b] = bank
-                    nc.tensor.matmul_mx(
-                        out=bank[:],
-                        lhsT=q_words[:, P * r : P * (r + 1)].bitcast(FP8X4),
-                        lhsT_scale=q_scales[:, P * r : P * (r + 1)],
-                        rhs=k_words[:, 512 * b : 512 * (b + 1)].bitcast(FP8X4),
-                        rhs_scale=k_scales[:, 512 * b : 512 * (b + 1)],
-                        start=True,
-                        stop=True,
-                    )
-            elif kind == "ev":
-                r, b = int(name[2]), int(name[3])
-                copy(who, a_sb[r][:, 512 * b : 512 * (b + 1)], banks[r, b][:])
-            elif kind in ("gx", "gy", "gz"):
-                r, h = int(name[2]), int(name[3])
-                n = "xyz".index(kind[1])
-                icopy(who, g[kind[1], r // 2, h][:, r % 2, :], a_sb[r][:].indirect(lists[n][:, 16 * h : 16 * (h + 1)]))
-            elif kind in ("hi", "lo"):
-                k, h = int(name[2]), int(name[3])
-                nc.vector.tensor_tensor(
-                    out=(hi if kind == "hi" else lo)[k, h][:, :, sl],
-                    in0=g["x", k, h][:, :, sl],
-                    in1=g["y", k, h][:, :, sl],
-                    op=ALU.max if kind == "hi" else ALU.min,
+        def gather(n, r, h, engine):
+            offsets = pick[n][:, LIST_COLS * h : LIST_COLS * (h + 1)]
+            move(engine, picked[n, r // 2, h][:, r % 2, :], a_sb[r][:].indirect(offsets))
+
+        def gather_pair(k, h, second_list_engine):
+            for r in (2 * k, 2 * k + 1):
+                gather(0, r, h, nc.scalar)
+                gather(1, r, h, second_list_engine)
+            for r in (2 * k, 2 * k + 1):
+                gather(2, r, h, nc.scalar)
+
+        def bounds(k, h):
+            nc.vector.tensor_tensor(out=hi[k, h][:], in0=picked[0, k, h][:], in1=picked[1, k, h][:], op=ALU.max)
+            nc.vector.tensor_tensor(out=lo[k, h][:], in0=picked[0, k, h][:], in1=picked[1, k, h][:], op=ALU.min)
+
+        def cap(k, h, slots):
+            nc.vector.tensor_tensor(out=hi[k, h][:, :, slots], in0=hi[k, h][:, :, slots], in1=picked[2, k, h][:, :, slots], op=ALU.min)
+
+        def middle(k, h, slots):
+            nc.vector.tensor_tensor(out=median[h][:, 2 * k : 2 * k + 2, slots], in0=lo[k, h][:, :, slots], in1=hi[k, h][:, :, slots], op=ALU.max)
+
+        def weigh(k, h, slots):
+            for r in (2 * k, 2 * k + 1):
+                nc.vector.tensor_scalar(
+                    out=wq[h][:, r, slots],
+                    in0=median[h][:, r, slots],
+                    scalar1=lam_sb[:, r : r + 1],
+                    scalar2=qs_sb[:, r : r + 1],
+                    op0=ALU.mult,
+                    op1=ALU.mult,
                 )
-            elif kind == "mi":
-                k, h = int(name[2]), int(name[3])
-                nc.vector.tensor_tensor(out=hi[k, h][:, :, sl], in0=hi[k, h][:, :, sl], in1=g["z", k, h][:, :, sl], op=ALU.min)
-            elif kind == "ww":
-                k, h = int(name[2]), int(name[3])
-                nc.vector.tensor_tensor(out=w[h][:, 2 * k : 2 * k + 2, sl], in0=lo[k, h][:, :, sl], in1=hi[k, h][:, :, sl], op=ALU.max)
-            elif kind == "sc":
-                h = int(name[2])
-                nc.vector.tensor_tensor(
-                    out=w_il[h][:, sl, :].rearrange("p (c i) t -> p c t i", i=4),
-                    in0=w[h][:, :, sl].rearrange("p t (c i) -> p c t i", i=4),
-                    in1=c_sb[:].unsqueeze(1).unsqueeze(3).to_broadcast([P, ns // 4, 4, 4]),
-                    op=ALU.mult,
-                )
-            elif kind == "ts":
-                r, h = int(name[2]), int(name[3])
-                nc.vector.tensor_scalar(out=w_bf[h][:, r, sl], in0=w[h][:, r, sl], scalar1=lam_sb[:, r : r + 1], scalar2=qs_sb[:, r : r + 1], op0=ALU.mult, op1=ALU.mult)
-            elif kind == "il":
-                h = int(name[2])
-                nc.vector.tensor_copy(out=w_il[h][:, sl, :].rearrange("p (c i) t -> p c t i", i=4), in_=w_bf[h][:, :, sl].rearrange("p t (c i) -> p c t i", i=4))
-            elif kind == "qw":
-                h = int(name[2])
-                nc.vector.quantize_mx(out=w_words[h][:, sl].bitcast(FP8X4), scales=w_scales[h][:, sl], in_=w_il[h][:, sl, :].rearrange("p i t -> p (i t)"))
-            elif kind == "ci":
-                es = slice(2 * sl.start, 2 * sl.stop)
-                copy(who, m_il[:, es, :].rearrange("p (c i) j -> p c j i", i=4), m_raw[:, :, es].rearrange("p j (c i) -> p c j i", i=4))
-            elif kind == "qm":
-                nc.vector.quantize_mx(out=m_words[:].bitcast(FP8X4), scales=m_scales[:], in_=m_il[:].rearrange("p e j -> p (e j)"))
-            elif kind == "m2":
-                h = int(name[2])
-                for k in range(2):
-                    bank = psd.tile([P, 2, H], F32, name="dbank")
-                    dbanks[k, h] = bank
-                    for u in range(2):
-                        e = 2 * k + u
-                        nc.tensor.matmul_mx(
-                            out=bank[:, u, :],
-                            lhsT=m_words[:, P * e : P * (e + 1)].bitcast(FP8X4),
-                            lhsT_scale=m_scales[:, P * e : P * (e + 1)],
-                            rhs=w_words[h][:].bitcast(FP8X4),
-                            rhs_scale=w_scales[h][:],
-                            start=True,
-                            stop=True,
-                        )
-            elif kind == "dl":
-                k, h = int(name[2]), int(name[3])
-                copy(who, dl[k, h][:], dbanks[k, h][:])
-            elif kind == "st":
-                e, h = int(name[2]), int(name[3])
-                a, b = (0, 16) if len(name) == 4 else ((0, 8) if name[4] == "a" else (8, 16))
-                icopy(who, wins[e][:].indirect(lists[3][:, 16 * h + a : 16 * h + b]), dl[e // 2, h][:, e % 2, 16 * a : 16 * b])
-            elif kind == "ad":
-                e = int(name[2])
-                a, b = (0, M) if len(name) == 3 else ((0, M // 2) if name[3] == "a" else (M // 2, M))
-                eng[who].tensor_tensor(out=olds[e][:, a:b], in0=olds[e][:, a:b], in1=wins[e][:, a:b], op=ALU.add)
-                nc.sync.dma_start(out=out[P * e : P * (e + 1), a:b], in_=olds[e][:, a:b])
+
+        def pack_weights(h, slots):
+            nc.vector.tensor_copy(
+                out=w_packed[h][:, slots, :].rearrange("p (c i) r -> p c r i", i=4),
+                in_=wq[h][:, :, slots].rearrange("p r (c i) -> p c r i", i=4),
+            )
+
+        def quantise_weights(h, slots):
+            nc.vector.quantize_mx(
+                out=w_words[h][:, slots].bitcast(FP8X4),
+                scales=w_scales[h][:, slots],
+                in_=w_packed[h][:, slots, :].rearrange("p i r -> p (i r)"),
+            )
+
+        def finish_half(h):
+            bounds(1, h)
+            for step in (cap, middle, weigh):
+                for slots in quarters:
+                    step(1, h, slots)
+            for step in (pack_weights, quantise_weights):
+                for slots in quarters:
+                    step(h, slots)
+            for k in pairs:
+                dl_bank[k, h] = psum.tile([P, 2, HALF], F32, name="bank")
+                for u in range(2):
+                    features = slice(P * (2 * k + u), P * (2 * k + u + 1))
+                    product(dl_bank[k, h][:, u, :], m_words[:, features], m_scales[:, features], w_words[h][:], w_scales[h][:])
+
+        def scatter(e, h, engine):
+            offsets = place[:, LIST_COLS * h : LIST_COLS * (h + 1)]
+            move(engine, window[e][:].indirect(offsets), dl[e // 2, h][:, e % 2, :])
+
+        def add_and_store(e, columns):
+            nc.vector.tensor_tensor(out=result[e][:, columns], in0=result[e][:, columns], in1=window[e][:, columns], op=ALU.add)
+            nc.sync.dma_start(out=out[P * e : P * (e + 1), columns], in_=result[e][:, columns])
+
+        scores(0)
+        scores(1)
+        for n in range(2):
+            nc.gpsimd.tensor_scalar(
+                out=m_packed[:, n * E // 2 : (n + 1) * E // 2, :],
+                in0=m_raw[n][:].rearrange("p j e -> p e j"),
+                scalar1=1.0,
+                scalar2=0.0,
+                op0=ALU.mult,
+                op1=ALU.add,
+            )
+        gather_pair(0, 0, nc.vector)
+        scores(2)
+        scores(3)
+        gather_pair(1, 0, nc.vector)
+        bounds(0, 0)
+        cap(0, 0, whole)
+        nc.vector.quantize_mx(out=m_words[:].bitcast(FP8X4), scales=m_scales[:], in_=m_packed[:].rearrange("p e j -> p (e j)"))
+        middle(0, 0, whole)
+        weigh(0, 0, whole)
+        finish_half(0)
+
+        gather_pair(0, 1, nc.scalar)
+        gather_pair(1, 1, nc.scalar)
+        bounds(0, 1)
+        cap(0, 1, whole)
+        middle(0, 1, whole)
+        weigh(0, 1, whole)
+        finish_half(1)
+
+        last = E_TILES - 1
+        for k in pairs:
+            nc.scalar.copy(out=dl[k, 0][:], in_=dl_bank[k, 0][:])
+        for e in range(E_TILES):
+            scatter(e, 0, nc.vector if e == last else nc.scalar)
+        for k in pairs:
+            nc.scalar.copy(out=dl[k, 1][:], in_=dl_bank[k, 1][:])
+        for e in range(E_TILES):
+            scatter(e, 1, nc.vector if e == 0 else nc.scalar)
+        for e in range(last):
+            add_and_store(e, slice(0, M))
+        add_and_store(last, slice(0, M // 2))
+        add_and_store(last, slice(M // 2, M))

@@ -64,7 +64,6 @@ def tile_attend_middle_deliveredplanes_lean_kernel(tc, query, keys_words, keys_s
         dl = {(k, h): keep.tile([P, 2, HALF], F32, name="dl%d%d" % (k, h)) for k in pairs for h in halves}
         dl_bank = {}
 
-        nc.gpsimd.memset(k_scales[:].bitcast(I32), 0)
         nc.sync.dma_start(out=q_raw[:], in_=query.rearrange("(p j) q -> p j q", j=PACK))
         for quad in range(4):
             nc.sync.dma_start(

from contextlib import ExitStack

import concourse.mybir as mybir

D, T, I, Q, E, M = 512, 1024, 512, 512, 512, 1024
FLOPS = 2 * D * Q * T + 2 * Q * E * I

F32 = mybir.dt.float32
BF16 = mybir.dt.bfloat16
U32 = mybir.dt.uint32
I32 = mybir.dt.int32
U16 = mybir.dt.uint16
U8 = mybir.dt.uint8
FP8X4 = mybir.dt.float8_e4m3fn_x4
ALU = mybir.AluOpType
COPY = mybir.ActivationFunctionType.Copy

P = 128
PACK = 4
BANK = 512
BANKS = 8
E_TILES = E // P
HALF = I // 2
LIST_COLS = HALF // 16
Q_GROUPS_VECTOR = 84


def tile_attend_middle_deliveredplanes_lean_kernel(tc, query, keys_words, keys_scales, lam, qs, msgs, old, offs, offs2, offs3, offs4, out):
    nc = tc.nc
    halves = range(2)
    pairs = range(2)
    whole = slice(0, HALF)
    quarters = (slice(0, HALF // 2), slice(HALF // 2, HALF))

    with ExitStack() as ctx:
        keep = ctx.enter_context(tc.tile_pool(name="keep", bufs=1))
        psum = ctx.enter_context(tc.psum_pool(name="psum", bufs=BANKS))

        pick = [keep.tile([P, I // 16], U16, name="pick%d" % n) for n in range(3)]
        place = keep.tile([P, I // 16], U16)
        k_words = keep.tile([P, T], U32, align_bytes=64)
        k_scales = keep.tile([P, T], U8, align_bytes=64)
        lam_sb = keep.tile([P, PACK], F32)
        qs_sb = keep.tile([P, PACK], F32)
        q_raw = keep.tile([P, PACK, Q], F32)
        q_packed = keep.tile([P, PACK, P, PACK], BF16, align_bytes=64)
        q_words = keep.tile([P, Q], U32, align_bytes=64)
        q_scales = keep.tile([P, Q], U8, align_bytes=64)
        m_raw = [keep.tile([P, PACK, E // 2], F32, name="m_raw%d" % n) for n in range(2)]
        m_packed = keep.tile([P, E, PACK], BF16, align_bytes=64)
        m_words = keep.tile([P, E], U32, align_bytes=64)
        m_scales = keep.tile([P, E], U8, align_bytes=64)
        result = [keep.tile([P, M], F32, name="result%d" % e) for e in range(E_TILES)]
        window = [keep.tile([P, M], F32, name="window%d" % e) for e in range(E_TILES)]
        a_sb = [keep.tile([P, T], F32, name="a%d" % r) for r in range(PACK)]
        picked = {(n, k, h): keep.tile([P, 2, HALF], F32, name="picked%d%d%d" % (n, k, h)) for n in range(3) for k in pairs for h in halves}
        lo = {(k, h): keep.tile([P, 2, HALF], F32, name="lo%d%d" % (k, h)) for k in pairs for h in halves}
        hi = {(k, h): keep.tile([P, 2, HALF], F32, name="hi%d%d" % (k, h)) for k in pairs for h in halves}
        median = [keep.tile([P, PACK, HALF], F32, name="median%d" % h) for h in halves]
        wq = [keep.tile([P, PACK, HALF], BF16, name="wq%d" % h) for h in halves]
        w_packed = [keep.tile([P, HALF, PACK], BF16, name="w_packed%d" % h, align_bytes=64) for h in halves]
        w_words = [keep.tile([P, HALF], U32, name="w_words%d" % h, align_bytes=64) for h in halves]
        w_scales = [keep.tile([P, HALF], U8, name="w_scales%d" % h, align_bytes=64) for h in halves]
        dl = {(k, h): keep.tile([P, 2, HALF], F32, name="dl%d%d" % (k, h)) for k in pairs for h in halves}
        dl_bank = {}

        nc.sync.dma_start(out=q_raw[:], in_=query.rearrange("(p j) q -> p j q", j=PACK))
        for quad in range(4):
            nc.sync.dma_start(
                out=k_scales[32 * quad : 32 * quad + 4, :].bitcast(I32),
                in_=keys_scales[0, 4 * quad : 4 * quad + 4, :].bitcast(I32),
            )
        nc.sync.dma_start(out=k_words[:].bitcast(I32), in_=keys_words[0].rearrange("p n t -> p (n t)").bitcast(I32))
        for tile, offsets in zip(pick, (offs, offs2, offs3)):
            nc.sync.dma_start(tile[:], offsets)
        m_rows = msgs.rearrange("(p j) e -> p j e", j=PACK)
        for n in range(2):
            nc.sync.dma_start(out=m_raw[n][:], in_=m_rows[:, :, n * E // 2 : (n + 1) * E // 2])
        nc.sync.dma_start(out=lam_sb[:], in_=lam.rearrange("(p r) o -> p (r o)", r=PACK))
        nc.sync.dma_start(out=qs_sb[:], in_=qs.rearrange("(p r) o -> p (r o)", r=PACK))
        nc.sync.dma_start(place[:], offs4)
        for e in range(E_TILES):
            nc.sync.dma_start(out=result[e][:], in_=old[P * e : P * (e + 1), :])
        for e in range(E_TILES):
            nc.vector.memset(window[e][:], 0.0)

        q_to = q_packed[:].rearrange("p r s j -> p s r j")
        q_from = q_raw[:].rearrange("p j (s r) -> p s r j", r=PACK)
        nc.vector.tensor_copy(out=q_to[:, :Q_GROUPS_VECTOR], in_=q_from[:, :Q_GROUPS_VECTOR])
        nc.scalar.activation(out=q_to[:, Q_GROUPS_VECTOR:], in_=q_from[:, Q_GROUPS_VECTOR:], func=COPY)
        for r in range(PACK):
            nc.vector.quantize_mx(
                out=q_words[:, P * r : P * (r + 1)].bitcast(FP8X4),
                scales=q_scales[:, P * r : P * (r + 1)],
                in_=q_packed[:, r, :, :].rearrange("p s j -> p (s j)"),
            )

        def product(bank, lhs_words, lhs_scales, rhs_words, rhs_scales):
            nc.tensor.matmul_mx(
                out=bank,
                lhsT=lhs_words.bitcast(FP8X4),
                lhsT_scale=lhs_scales,
                rhs=rhs_words.bitcast(FP8X4),
                rhs_scale=rhs_scales,
                start=True,
                stop=True,
            )

        def move(engine, to, source):
            if engine is nc.scalar:
                nc.scalar.activation(out=to, in_=source, func=COPY)
            else:
                nc.vector.tensor_copy(out=to, in_=source)

        def scores(r):
            rows = slice(P * r, P * (r + 1))
            banks = []
            for b in range(T // BANK):
                tokens = slice(BANK * b, BANK * (b + 1))
                bank = psum.tile([P, BANK], F32, name="bank")
                product(bank[:], q_words[:, rows], q_scales[:, rows], k_words[:, tokens], k_scales[:, tokens])
                banks.append(bank)
            nc.scalar.copy(out=a_sb[r][:, :BANK], in_=banks[0][:])
            nc.vector.tensor_copy(out=a_sb[r][:, BANK:], in_=banks[1][:])

        def gather(n, r, h, engine):
            offsets = pick[n][:, LIST_COLS * h : LIST_COLS * (h + 1)]
            move(engine, picked[n, r // 2, h][:, r % 2, :], a_sb[r][:].indirect(offsets))

        def gather_pair(k, h, second_list_engine):
            for r in (2 * k, 2 * k + 1):
                gather(0, r, h, nc.scalar)
                gather(1, r, h, second_list_engine)
            for r in (2 * k, 2 * k + 1):
                gather(2, r, h, nc.scalar)

        def bounds(k, h):
            nc.vector.tensor_tensor(out=hi[k, h][:], in0=picked[0, k, h][:], in1=picked[1, k, h][:], op=ALU.max)
            nc.vector.tensor_tensor(out=lo[k, h][:], in0=picked[0, k, h][:], in1=picked[1, k, h][:], op=ALU.min)

        def cap(k, h, slots):
            nc.vector.tensor_tensor(out=hi[k, h][:, :, slots], in0=hi[k, h][:, :, slots], in1=picked[2, k, h][:, :, slots], op=ALU.min)

        def middle(k, h, slots):
            nc.vector.tensor_tensor(out=median[h][:, 2 * k : 2 * k + 2, slots], in0=lo[k, h][:, :, slots], in1=hi[k, h][:, :, slots], op=ALU.max)

        def weigh(k, h, slots):
            for r in (2 * k, 2 * k + 1):
                nc.vector.tensor_scalar(
                    out=wq[h][:, r, slots],
                    in0=median[h][:, r, slots],
                    scalar1=lam_sb[:, r : r + 1],
                    scalar2=qs_sb[:, r : r + 1],
                    op0=ALU.mult,
                    op1=ALU.mult,
                )

        def pack_weights(h, slots):
            nc.vector.tensor_copy(
                out=w_packed[h][:, slots, :].rearrange("p (c i) r -> p c r i", i=4),
                in_=wq[h][:, :, slots].rearrange("p r (c i) -> p c r i", i=4),
            )

        def quantise_weights(h, slots):
            nc.vector.quantize_mx(
                out=w_words[h][:, slots].bitcast(FP8X4),
                scales=w_scales[h][:, slots],
                in_=w_packed[h][:, slots, :].rearrange("p i r -> p (i r)"),
            )

        def finish_half(h):
            bounds(1, h)
            for step in (cap, middle, weigh):
                for slots in quarters:
                    step(1, h, slots)
            for step in (pack_weights, quantise_weights):
                for slots in quarters:
                    step(h, slots)
            for k in pairs:
                dl_bank[k, h] = psum.tile([P, 2, HALF], F32, name="bank")
                for u in range(2):
                    features = slice(P * (2 * k + u), P * (2 * k + u + 1))
                    product(dl_bank[k, h][:, u, :], m_words[:, features], m_scales[:, features], w_words[h][:], w_scales[h][:])

        def scatter(e, h, engine):
            offsets = place[:, LIST_COLS * h : LIST_COLS * (h + 1)]
            move(engine, window[e][:].indirect(offsets), dl[e // 2, h][:, e % 2, :])

        def add_and_store(e, columns):
            nc.vector.tensor_tensor(out=result[e][:, columns], in0=result[e][:, columns], in1=window[e][:, columns], op=ALU.add)
            nc.sync.dma_start(out=out[P * e : P * (e + 1), columns], in_=result[e][:, columns])

        scores(0)
        scores(1)
        for n in range(2):
            nc.gpsimd.tensor_scalar(
                out=m_packed[:, n * E // 2 : (n + 1) * E // 2, :],
                in0=m_raw[n][:].rearrange("p j e -> p e j"),
                scalar1=1.0,
                scalar2=0.0,
                op0=ALU.mult,
                op1=ALU.add,
            )
        gather_pair(0, 0, nc.vector)
        scores(2)
        scores(3)
        gather_pair(1, 0, nc.vector)
        bounds(0, 0)
        cap(0, 0, whole)
        nc.vector.quantize_mx(out=m_words[:].bitcast(FP8X4), scales=m_scales[:], in_=m_packed[:].rearrange("p e j -> p (e j)"))
        middle(0, 0, whole)
        weigh(0, 0, whole)
        finish_half(0)

        gather_pair(0, 1, nc.scalar)
        gather_pair(1, 1, nc.scalar)
        bounds(0, 1)
        cap(0, 1, whole)
        middle(0, 1, whole)
        weigh(0, 1, whole)
        finish_half(1)

        last = E_TILES - 1
        for k in pairs:
            nc.scalar.copy(out=dl[k, 0][:], in_=dl_bank[k, 0][:])
        for e in range(E_TILES):
            scatter(e, 0, nc.vector if e == last else nc.scalar)
        for k in pairs:
            nc.scalar.copy(out=dl[k, 1][:], in_=dl_bank[k, 1][:])
        for e in range(E_TILES):
            scatter(e, 1, nc.vector if e == 0 else nc.scalar)
        for e in range(last):
            add_and_store(e, slice(0, M))
        add_and_store(last, slice(0, M // 2))
        add_and_store(last, slice(M // 2, M))
